import numpy as np
import ml_dtypes


def mxq(x, axis, fmt="e4m3"):
    dtype, down = {"e4m3": (ml_dtypes.float8_e4m3fn, 7), "e5m2": (ml_dtypes.float8_e5m2, 14)}[fmt]
    v = np.moveaxis(np.asarray(x, np.float32).astype(ml_dtypes.bfloat16).astype(np.float64), axis, -1)
    blocks = v.reshape(v.shape[:-1] + (-1, 32))
    amax = np.abs(blocks).max(-1, keepdims=True)
    byte = np.maximum(np.where(amax > 0, np.frexp(amax)[1] - 1 + 127, 0) - down, 1)
    scale = np.exp2(byte - 127.0)
    codes = (blocks / scale).astype(np.float32).astype(dtype).astype(np.float64)
    return np.moveaxis((codes * scale).reshape(v.shape), -1, axis)


WIDE = False


def mx_kscale(k):
    if not WIDE:
        return np.ones(k)
    levels = np.array([10, -10, 5, -5, 0])
    if k % 512:
        return np.exp2(np.random.permutation(np.resize(levels, k // 32))).repeat(32)
    a = np.empty((k // 512, 16))
    for p in range(k // 512):
        a[p, :8] = np.random.permutation(np.resize(levels, 8))
        for g in range(8):
            far = levels[np.abs(levels - a[p, g]) >= 10]
            a[p, g + 8] = far[np.random.randint(len(far))]
    return np.exp2(a.ravel()).repeat(32)


def f64(x):
    return np.asarray(x).astype(np.float64)


def striped(idx):
    return np.tile(idx.reshape(-1, 16).T, (8, 1)).astype(np.uint16)


def unstriped(offs):
    return offs[:16].T.reshape(-1).astype(np.int64)


def gelu(v):
    return 0.5 * v * (1.0 + np.tanh(np.sqrt(2.0 / np.pi) * (v + 0.044715 * v**3)))


K, T, D, V, H, N = 2048, 1024, 6, 512, 512, 128
P = 2 ** 7


def setup_inputs():
    n = np.random.standard_normal
    s = mx_kscale(K)[:, None]
    u = mx_kscale(H)
    return {
        "xT": (n((K, T)) * s).astype(np.float32),
        "w1": (n((K, H)) / np.sqrt(K) / s * u).astype(np.float32),
        "w2": (n((H, N)) / np.sqrt(H) / u[:, None]).astype(np.float32),
        "gate": np.tile(np.random.uniform(0.2, 1.0, (D, 1, V)) / np.sqrt(D), (1, P, 1)).astype(np.float32),
        "pos1": striped(np.random.permutation(T)[:V]),
        "pos2": striped(np.random.permutation(T)[:V]),
        "pos3": striped(np.random.permutation(T)[:V]),
        "pos4": striped(np.random.permutation(T)[:V]),
        "pos5": striped(np.random.permutation(T)[:V]),
        "pos6": striped(np.random.permutation(T)[:V]),
    }


def reference(xT, w1, w2, gate, pos1, pos2, pos3, pos4, pos5, pos6):
    h = gelu(mxq(f64(w1), 0, "e4m3").T @ mxq(f64(xT), 0, "e4m3"))
    z = sum(f64(gate)[d, :1] * h[:, unstriped(p)] for d, p in enumerate((pos1, pos2, pos3, pos4, pos5, pos6)))
    return mxq(f64(w2), 0, "e4m3").T @ mxq(z, 0, "e4m3")

@@ -1,0 +1,238 @@
+from contextlib import ExitStack
+
+import concourse.mybir as mybir
+from concourse.masks import make_identity
+
+K, T, D, V, H, N = 2048, 1024, 6, 512, 512, 128
+FLOPS = 2 * K * H * T + 2 * H * N * V
+BYTES = 4 * (K * T + K * H + H * N + D * V + N * V) + 2 * D * 128 * (V // 16)
+
+F32 = mybir.dt.float32
+BF16 = mybir.dt.bfloat16
+U32 = mybir.dt.uint32
+U16 = mybir.dt.uint16
+U8 = mybir.dt.uint8
+FP8X4 = mybir.dt.float8_e4m3fn_x4
+MULT = mybir.AluOpType.mult
+GELU = mybir.ActivationFunctionType.Gelu_apprx_tanh
+
+P = 128
+PACK = 4
+KP = P * PACK
+PASSES = K // KP
+BLOCKS = H // P
+CHUNKS = V // P
+
+LAST_PIECES = ((0, 512), (512, 768), (768, 896), (896, 1024))
+BANK_COLS = LAST_PIECES
+QUANT = {(0, 384): ((0, 256), (256, 384)), (384, 512): ((384, 512),)}
+V_PIECES = {0: ((0, 512),), 1: ((0, 512),), 2: ((0, 512),), 3: ((0, 384), (384, 512))}
+
+
+def tile_picked_gcn_mlp_gelu_sub_l_kernel(tc, xT, w1, w2, gate, pos1, pos2, pos3, pos4, pos5, pos6, out):
+    nc = tc.nc
+    lists = (pos1, pos2, pos3, pos4, pos5, pos6)
+
+    def interleave(copy, dst, raw):
+        copy(
+            out=dst.rearrange("p (c i) j -> p c j i", i=4),
+            in_=raw.rearrange("p j (c i) -> p c j i", i=4),
+        )
+
+    def quantize(codes, scales, bf):
+        nc.vector.quantize_mx(out=codes.bitcast(FP8X4), scales=scales, in_=bf)
+
+    with ExitStack() as ctx:
+        keep = ctx.enter_context(tc.tile_pool(name="keep", bufs=1))
+        stage = ctx.enter_context(tc.tile_pool(name="stage", bufs=3))
+        gpool = ctx.enter_context(tc.tile_pool(name="gpool", bufs=8))
+        psum = ctx.enter_context(tc.psum_pool(name="psum", bufs=1))
+
+        offsets = [keep.tile([P, V // 16], U16, name=f"offsets{d}") for d in range(D)]
+        ident = keep.tile([P, P], F32, name="ident")
+        ident_bf = keep.tile([P, P], BF16, name="ident_bf")
+        warm = keep.tile([P, 1], F32, name="warm")
+        warm_out = keep.tile([P, 1], F32, name="warm_out")
+        gate_rows = keep.tile([P, V], F32, name="gate_rows")
+        gate_cols = keep.tile([P, CHUNKS, D], F32, name="gate_cols")
+        gates = [keep.tile([P, V], F32, name=f"gate{d}") for d in range(D)]
+
+        x_raw = [keep.tile([P, PACK, T], F32, name=f"x_raw{c}") for c in range(PASSES)]
+        x_codes = [keep.tile([P, T], U32, name=f"x_codes{c}", align_bytes=64) for c in range(PASSES)]
+        x_scales = [keep.tile([P, T], U8, name=f"x_scales{c}", align_bytes=64) for c in range(PASSES)]
+
+        groups = ((0, 128), (128, 128), (256, 256))
+        w1_raw = [[keep.tile([P, PACK, w], F32, name=f"w1_raw{g}_{c}") for c in range(PASSES)] for g, (a, w) in enumerate(groups)]
+        w1_bf = [keep.tile([P, PASSES, w, PACK], BF16, name=f"w1_bf{g}", align_bytes=64) for g, (a, w) in enumerate(groups)]
+        w1_codes = [keep.tile([P, PASSES, w], U32, name=f"w1_codes{g}", align_bytes=64) for g, (a, w) in enumerate(groups)]
+        w1_scales = [keep.tile([P, PASSES, w], U8, name=f"w1_scales{g}", align_bytes=64) for g, (a, w) in enumerate(groups)]
+        w2_raw = keep.tile([P, PACK, N], F32, name="w2_raw")
+        w2_bf = keep.tile([P, N, PACK], BF16, name="w2_bf", align_bytes=64)
+        w2_codes = keep.tile([P, N], U32, name="w2_codes", align_bytes=64)
+        w2_scales = keep.tile([P, N], U8, name="w2_scales", align_bytes=64)
+        zt_sb = [keep.tile([P, PACK, P], BF16, name=f"zt_sb{c}") for c in range(CHUNKS)]
+        z_bf = keep.tile([P, V, PACK], BF16, name="z_bf", align_bytes=64)
+        z_codes = keep.tile([P, V], U32, name="z_codes", align_bytes=64)
+        z_scales = keep.tile([P, V], U8, name="z_scales", align_bytes=64)
+        out_sb = keep.tile([P, V], F32, name="out_sb")
+
+        def load_w1(g):
+            a, w = groups[g]
+            for c in range(PASSES):
+                nc.sync.dma_start(out=w1_raw[g][c][:], in_=w1[c * KP : (c + 1) * KP, a : a + w].rearrange("(p j) i -> p j i", j=PACK))
+
+        def load_x(c, a, b):
+            nc.sync.dma_start(out=x_raw[c][:, :, a:b], in_=xT[c * KP : (c + 1) * KP, a:b].rearrange("(p j) t -> p j t", j=PACK))
+
+        def load_list(d):
+            nc.sync.dma_start(offsets[d][:], lists[d])
+
+        nc.vector.memset(gate_rows[:], 0.0)
+        nc.gpsimd.memset(warm[:], 0.0)
+        nc.scalar.activation(out=warm_out[:], in_=warm[:], func=GELU)
+        nc.sync.dma_start(out=gate_rows[0:4, :], in_=gate[0:4, 0, :])
+        nc.sync.dma_start(out=gate_rows[4:6, :], in_=gate[4:6, 0, :])
+        make_identity(nc, ident[:])
+        nc.gpsimd.tensor_copy(out=ident_bf[:], in_=ident[:])
+
+        load_w1(0)
+        load_x(0, 0, T)
+        load_x(1, 0, T)
+        load_list(0)
+        load_x(2, 0, T)
+        for a, b in LAST_PIECES:
+            load_x(3, a, b)
+        for d in range(1, D):
+            load_list(d)
+        load_w1(1)
+        load_w1(2)
+        nc.sync.dma_start(out=w2_raw[:], in_=w2.rearrange("(p j) m -> p j m", j=PACK))
+
+        turned = psum.tile([P, CHUNKS, P], F32, name="turned", tag="zt0")
+        for c in range(CHUNKS):
+            nc.tensor.transpose(out=turned[:, c, :], in_=gate_rows[:, c * P : (c + 1) * P], identity=ident[:])
+        nc.vector.tensor_copy(out=gate_cols[:], in_=turned[:, :, 0:D])
+        for d in range(D):
+            spread = psum.tile([P, CHUNKS, P], F32, name=f"spread{d}", tag=f"zt{(d + 1) % 4}")
+            for c in range(CHUNKS):
+                nc.tensor.transpose(out=spread[:, c, :], in_=gate_cols[:, c, d : d + 1].to_broadcast([P, P]), identity=ident[:])
+            nc.scalar.copy(out=gates[d][:], in_=spread[:].rearrange("p c v -> p (c v)"))
+
+        def weights(g, copy):
+            step = 512 // groups[g][1]
+            for c0 in range(0, PASSES, step):
+                cs = slice(c0, c0 + step)
+                for c in range(c0, c0 + step):
+                    interleave(copy, w1_bf[g][:, c], w1_raw[g][c][:])
+                quantize(
+                    w1_codes[g][:, cs].rearrange("p c i -> p (c i)"),
+                    w1_scales[g][:, cs].rearrange("p c i -> p (c i)"),
+                    w1_bf[g][:, cs].rearrange("p c i j -> p (c i j)"),
+                )
+
+        weights(0, nc.scalar.copy)
+
+        banks0 = [psum.tile([P, 512], F32, name=f"h0_{i}", tag=t) for i, t in enumerate(("hA", "hB", "back", "outb"))]
+
+        def product(bank, width, g, off, c, a):
+            nc.tensor.matmul_mx(
+                out=bank[:, 0:width],
+                lhsT=w1_codes[g][:, c, off : off + P].bitcast(FP8X4),
+                lhsT_scale=w1_scales[g][:, c, off : off + P],
+                rhs=x_codes[c][:, a : a + width].bitcast(FP8X4),
+                rhs_scale=x_scales[c][:, a : a + width],
+                start=(c == 0),
+                stop=(c == PASSES - 1),
+            )
+
+        for c in range(PASSES):
+            x_bf = stage.tile([P, T, PACK], BF16, name=f"x_bf{c}", tag="x_bf", align_bytes=64)
+            flat = x_bf[:].rearrange("p t j -> p (t j)")
+            if c < PASSES - 1:
+                casts = ((nc.vector.tensor_copy, 0, 256), (nc.vector.tensor_copy, 256, 512), (nc.scalar.copy, 768, 1024), (nc.vector.tensor_copy, 512, 768))
+                if c == 0:
+                    casts = ((nc.vector.tensor_copy, 0, 256), (nc.scalar.copy, 256, 512), (nc.vector.tensor_copy, 512, 768), (nc.scalar.copy, 768, 1024))
+                for copy, a, b in casts:
+                    interleave(copy, x_bf[:, a:b, :], x_raw[c][:, :, a:b])
+                for a, b in ((0, 512), (512, 1024)):
+                    quantize(x_codes[c][:, a:b], x_scales[c][:, a:b], flat[:, PACK * a : PACK * b])
+            else:
+                for a, b in LAST_PIECES:
+                    m = a + (b - a) * 5 // 8
+                    interleave(nc.vector.tensor_copy, x_bf[:, a:m, :], x_raw[c][:, :, a:m])
+                    interleave(nc.scalar.copy, x_bf[:, m:b, :], x_raw[c][:, :, m:b])
+                    quantize(x_codes[c][:, a:b], x_scales[c][:, a:b], flat[:, PACK * a : PACK * b])
+            for bank, (a, b) in zip(banks0, BANK_COLS):
+                product(bank, b - a, 0, 0, c, a)
+
+        h = [keep.tile([P, T], F32, name=f"h{b}") for b in range(BLOCKS)]
+        for bank, (a, b) in zip(banks0, BANK_COLS):
+            nc.scalar.activation(out=h[0][:, a:b], in_=bank[:, 0 : b - a], func=GELU)
+
+        weights(1, nc.scalar.copy)
+        weights(2, nc.scalar.copy)
+        interleave(nc.scalar.copy, w2_bf[:], w2_raw[:])
+        quantize(w2_codes[:], w2_scales[:], w2_bf[:].rearrange("p m j -> p (m j)"))
+        for b in range(1, BLOCKS):
+            g, off = ((1, 0), (2, 0), (2, P))[b - 1]
+            for i, t in enumerate(("hA", "hB")):
+                bank = psum.tile([P, 512], F32, name=f"h{b}_{i}", tag=t)
+                for c in range(PASSES):
+                    product(bank, 512, g, off, c, 512 * i)
+                nc.scalar.activation(out=h[b][:, 512 * i : 512 * (i + 1)], in_=bank[:], func=GELU)
+
+        zt = [psum.tile([P, H], F32, name=f"zt_{c}", tag=f"zt{c}") for c in range(CHUNKS)]
+
+        def turn_back(c, tag, copies):
+            back = psum.tile([P, PACK, P], BF16, name=f"back{c}", tag=tag)
+            for t in range(PACK):
+                nc.tensor.transpose(out=back[:, t, :], in_=zt_sb[c][:, t, :], identity=ident_bf[:])
+            step = P // len(copies)
+            for i, copy in enumerate(copies):
+                interleave(copy, z_bf[:, c * P + i * step : c * P + (i + 1) * step, :], back[:, :, i * step : (i + 1) * step])
+
+        def finish(a, e, copy):
+            quantize(z_codes[:, a:e], z_scales[:, a:e], z_bf[:, a:e, :].rearrange("p v j -> p (v j)"))
+            nc.tensor.matmul_mx(
+                out=out_bank[:, a:e],
+                lhsT=w2_codes[:].bitcast(FP8X4),
+                lhsT_scale=w2_scales[:],
+                rhs=z_codes[:, a:e].bitcast(FP8X4),
+                rhs_scale=z_scales[:, a:e],
+                start=True,
+                stop=True,
+            )
+            copy(out=out_sb[:, a:e], in_=out_bank[:, a:e])
+
+        back_tags = ("back", "hA", "hB", "back")
+        for b in range(BLOCKS):
+            for a, e in V_PIECES[b]:
+                for d in range(D):
+                    picked = gpool.tile([P, e - a], F32, name=f"picked{b}_{a}_{d}", tag="picked")
+                    offs = offsets[d][:] if e - a == V else offsets[d][:, a // 16 : e // 16]
+                    nc.vector.tensor_tensor(picked[:], h[b][:].indirect(offs), gates[d][:, a:e], MULT)
+                    for c in range(a // P, e // P):
+                        nc.tensor.matmul(
+                            zt[c][:, b * P : (b + 1) * P],
+                            picked[:, c * P - a : (c + 1) * P - a],
+                            ident[:],
+                            start=(d == 0),
+                            stop=(d == D - 1),
+                            is_transpose=True,
+                        )
+                if b == BLOCKS - 2:
+                    for c in range(CHUNKS):
+                        done = (BLOCKS - 1) * P
+                        nc.scalar.copy(out=zt_sb[c][:, :, 0 : done // PACK], in_=zt[c][:, 0:done].rearrange("v (p t) -> v t p", t=PACK))
+                if b == BLOCKS - 1:
+                    if a == 0:
+                        out_bank = psum.tile([P, V], F32, name="out_bank", tag="outb")
+                    done = (BLOCKS - 1) * P
+                    last = e == V
+                    for c in range(a // P, e // P):
+                        rest = nc.vector.tensor_copy if last else nc.scalar.copy
+                        rest(out=zt_sb[c][:, :, done // PACK : P], in_=zt[c][:, done:H].rearrange("v (p t) -> v t p", t=PACK))
+                        turn_back(c, back_tags[c], (nc.vector.tensor_copy, nc.scalar.copy) if last else (nc.scalar.copy,))
+                    for q0, q1 in QUANT[(a, e)]:
+                        finish(q0, q1, nc.vector.tensor_copy if last else nc.scalar.copy)
+                    nc.sync.dma_start(out=out[:, a:e], in_=out_sb[:, a:e])

@@ -25,8 +25,10 @@ CHUNKS = V // P
 
 LAST_PIECES = ((0, 512), (512, 768), (768, 896), (896, 1024))
 BANK_COLS = LAST_PIECES
-QUANT = {(0, 384): ((0, 256), (256, 384)), (384, 512): ((384, 512),)}
-V_PIECES = {0: ((0, 512),), 1: ((0, 512),), 2: ((0, 512),), 3: ((0, 384), (384, 512))}
+QUANTIZE_AFTER = {(0, 1): ((1, 0, 2),), (0, 2): ((1, 2, 2),), (1, 0): ((2, 0, 2),), (1, 2): ((2, 2, 2),)}
+MULTIPLY_AFTER = {(0, 1): ((0, 2),), (0, 2): ((2, 2),), (1, 0): ((0, 2),), (1, 2): ((2, 2),), (2, 0): ((0, 4),)}
+SPLIT = 384
+FIRST_QUANTS = ((0, 256), (256, 384))
 
 
 def tile_picked_gcn_mlp_gelu_sub_l_kernel(tc, xT, w1, w2, gate, pos1, pos2, pos3, pos4, pos5, pos6, out):
@@ -76,10 +78,9 @@ def tile_picked_gcn_mlp_gelu_sub_l_kernel(tc, xT, w1, w2, gate, pos1, pos2, pos3
         z_scales = keep.tile([P, V], U8, name="z_scales", align_bytes=64)
         out_sb = keep.tile([P, V], F32, name="out_sb")
 
-        def load_w1(g):
+        def load_w1(g, c):
             a, w = groups[g]
-            for c in range(PASSES):
-                nc.sync.dma_start(out=w1_raw[g][c][:], in_=w1[c * KP : (c + 1) * KP, a : a + w].rearrange("(p j) i -> p j i", j=PACK))
+            nc.sync.dma_start(out=w1_raw[g][c][:], in_=w1[c * KP : (c + 1) * KP, a : a + w].rearrange("(p j) i -> p j i", j=PACK))
 
         def load_x(c, a, b):
             nc.sync.dma_start(out=x_raw[c][:, :, a:b], in_=xT[c * KP : (c + 1) * KP, a:b].rearrange("(p j) t -> p j t", j=PACK))
@@ -90,22 +91,29 @@ def tile_picked_gcn_mlp_gelu_sub_l_kernel(tc, xT, w1, w2, gate, pos1, pos2, pos3
         nc.vector.memset(gate_rows[:], 0.0)
         nc.gpsimd.memset(warm[:], 0.0)
         nc.scalar.activation(out=warm_out[:], in_=warm[:], func=GELU)
-        nc.sync.dma_start(out=gate_rows[0:4, :], in_=gate[0:4, 0, :])
-        nc.sync.dma_start(out=gate_rows[4:6, :], in_=gate[4:6, 0, :])
         make_identity(nc, ident[:])
         nc.gpsimd.tensor_copy(out=ident_bf[:], in_=ident[:])
 
-        load_w1(0)
+        for c in range(PASSES):
+            load_w1(0, c)
+        nc.sync.dma_start(out=gate_rows[0:4, :], in_=gate[0:4, 0, :])
+        nc.sync.dma_start(out=gate_rows[4:6, :], in_=gate[4:6, 0, :])
         load_x(0, 0, T)
         load_x(1, 0, T)
         load_list(0)
         load_x(2, 0, T)
         for a, b in LAST_PIECES:
             load_x(3, a, b)
-        for d in range(1, D):
+        load_w1(1, 0)
+        load_w1(1, 1)
+        load_list(1)
+        load_w1(1, 2)
+        load_list(2)
+        load_w1(1, 3)
+        for d in range(3, D):
             load_list(d)
-        load_w1(1)
-        load_w1(2)
+        for c in range(PASSES):
+            load_w1(2, c)
         nc.sync.dma_start(out=w2_raw[:], in_=w2.rearrange("(p j) m -> p j m", j=PACK))
 
         turned = psum.tile([P, CHUNKS, P], F32, name="turned", tag="zt0")
@@ -118,19 +126,21 @@ def tile_picked_gcn_mlp_gelu_sub_l_kernel(tc, xT, w1, w2, gate, pos1, pos2, pos3
                 nc.tensor.transpose(out=spread[:, c, :], in_=gate_cols[:, c, d : d + 1].to_broadcast([P, P]), identity=ident[:])
             nc.scalar.copy(out=gates[d][:], in_=spread[:].rearrange("p c v -> p (c v)"))
 
-        def weights(g, copy):
-            step = 512 // groups[g][1]
-            for c0 in range(0, PASSES, step):
-                cs = slice(c0, c0 + step)
-                for c in range(c0, c0 + step):
-                    interleave(copy, w1_bf[g][:, c], w1_raw[g][c][:])
-                quantize(
-                    w1_codes[g][:, cs].rearrange("p c i -> p (c i)"),
-                    w1_scales[g][:, cs].rearrange("p c i -> p (c i)"),
-                    w1_bf[g][:, cs].rearrange("p c i j -> p (c i j)"),
-                )
+        def quantize_w1(g, c0, n):
+            cs = slice(c0, c0 + n)
+            quantize(
+                w1_codes[g][:, cs].rearrange("p c i -> p (c i)"),
+                w1_scales[g][:, cs].rearrange("p c i -> p (c i)"),
+                w1_bf[g][:, cs].rearrange("p c i j -> p (c i j)"),
+            )
 
-        weights(0, nc.scalar.copy)
+        def cast_w1(g):
+            for c in range(PASSES):
+                interleave(nc.scalar.copy, w1_bf[g][:, c], w1_raw[g][c][:])
+
+        cast_w1(0)
+        quantize_w1(0, 0, 2)
+        quantize_w1(0, 2, 2)
 
         banks0 = [psum.tile([P, 512], F32, name=f"h0_{i}", tag=t) for i, t in enumerate(("hA", "hB", "back", "outb"))]
 
@@ -158,9 +168,10 @@ def tile_picked_gcn_mlp_gelu_sub_l_kernel(tc, xT, w1, w2, gate, pos1, pos2, pos3
                     quantize(x_codes[c][:, a:b], x_scales[c][:, a:b], flat[:, PACK * a : PACK * b])
             else:
                 for a, b in LAST_PIECES:
-                    m = a + (b - a) * 5 // 8
+                    m = b if b - a == P else a + (b - a) * 5 // 8
                     interleave(nc.vector.tensor_copy, x_bf[:, a:m, :], x_raw[c][:, :, a:m])
-                    interleave(nc.scalar.copy, x_bf[:, m:b, :], x_raw[c][:, :, m:b])
+                    if m < b:
+                        interleave(nc.scalar.copy, x_bf[:, m:b, :], x_raw[c][:, :, m:b])
                     quantize(x_codes[c][:, a:b], x_scales[c][:, a:b], flat[:, PACK * a : PACK * b])
             for bank, (a, b) in zip(banks0, BANK_COLS):
                 product(bank, b - a, 0, 0, c, a)
@@ -169,17 +180,20 @@ def tile_picked_gcn_mlp_gelu_sub_l_kernel(tc, xT, w1, w2, gate, pos1, pos2, pos3
         for bank, (a, b) in zip(banks0, BANK_COLS):
             nc.scalar.activation(out=h[0][:, a:b], in_=bank[:, 0 : b - a], func=GELU)
 
-        weights(1, nc.scalar.copy)
-        weights(2, nc.scalar.copy)
+        cast_w1(1)
+        cast_w1(2)
         interleave(nc.scalar.copy, w2_bf[:], w2_raw[:])
-        quantize(w2_codes[:], w2_scales[:], w2_bf[:].rearrange("p m j -> p (m j)"))
-        for b in range(1, BLOCKS):
-            g, off = ((1, 0), (2, 0), (2, P))[b - 1]
-            for i, t in enumerate(("hA", "hB")):
-                bank = psum.tile([P, 512], F32, name=f"h{b}_{i}", tag=t)
-                for c in range(PASSES):
+
+        def start_block(b):
+            return [psum.tile([P, 512], F32, name=f"h{b}_{i}", tag=t) for i, t in enumerate(("hA", "hB"))]
+
+        def multiply_block(b, banks, c0, n):
+            g, off = ((0, 0), (1, 0), (2, 0), (2, P))[b]
+            for c in range(c0, c0 + n):
+                for i, bank in enumerate(banks):
                     product(bank, 512, g, off, c, 512 * i)
-                nc.scalar.activation(out=h[b][:, 512 * i : 512 * (i + 1)], in_=bank[:], func=GELU)
+                    if c == PASSES - 1:
+                        nc.scalar.activation(out=h[b][:, 512 * i : 512 * (i + 1)], in_=bank[:], func=GELU)
 
         zt = [psum.tile([P, H], F32, name=f"zt_{c}", tag=f"zt{c}") for c in range(CHUNKS)]
 
@@ -204,35 +218,50 @@ def tile_picked_gcn_mlp_gelu_sub_l_kernel(tc, xT, w1, w2, gate, pos1, pos2, pos3
             )
             copy(out=out_sb[:, a:e], in_=out_bank[:, a:e])
 
+        def gather(b, a, e, d):
+            picked = gpool.tile([P, e - a], F32, name=f"picked{b}_{a}_{d}", tag="picked")
+            offs = offsets[d][:] if e - a == V else offsets[d][:, a // 16 : e // 16]
+            nc.vector.tensor_tensor(picked[:], h[b][:].indirect(offs), gates[d][:, a:e], MULT)
+            for c in range(a // P, e // P):
+                nc.tensor.matmul(
+                    zt[c][:, b * P : (b + 1) * P],
+                    picked[:, c * P - a : (c + 1) * P - a],
+                    ident[:],
+                    start=(d == 0),
+                    stop=(d == D - 1),
+                    is_transpose=True,
+                )
+
+        def round_sums(copy, c, a, e):
+            copy(out=zt_sb[c][:, :, a // PACK : e // PACK], in_=zt[c][:, a:e].rearrange("v (p t) -> v t p", t=PACK))
+
+        for b in range(BLOCKS - 1):
+            nb = start_block(b + 1)
+            for d in range(D):
+                gather(b, 0, V, d)
+                for g, c0, n in QUANTIZE_AFTER.get((b, d), ()):
+                    quantize_w1(g, c0, n)
+                for c0, n in MULTIPLY_AFTER.get((b, d), ()):
+                    multiply_block(b + 1, nb, c0, n)
+        quantize(w2_codes[:], w2_scales[:], w2_bf[:].rearrange("p m j -> p (m j)"))
+
+        done = (BLOCKS - 1) * P
+        for c in range(CHUNKS):
+            round_sums(nc.scalar.copy, c, 0, done)
+        out_bank = psum.tile([P, V], F32, name="out_bank", tag="outb")
         back_tags = ("back", "hA", "hB", "back")
-        for b in range(BLOCKS):
-            for a, e in V_PIECES[b]:
-                for d in range(D):
-                    picked = gpool.tile([P, e - a], F32, name=f"picked{b}_{a}_{d}", tag="picked")
-                    offs = offsets[d][:] if e - a == V else offsets[d][:, a // 16 : e // 16]
-                    nc.vector.tensor_tensor(picked[:], h[b][:].indirect(offs), gates[d][:, a:e], MULT)
-                    for c in range(a // P, e // P):
-                        nc.tensor.matmul(
-                            zt[c][:, b * P : (b + 1) * P],
-                            picked[:, c * P - a : (c + 1) * P - a],
-                            ident[:],
-                            start=(d == 0),
-                            stop=(d == D - 1),
-                            is_transpose=True,
-                        )
-                if b == BLOCKS - 2:
-                    for c in range(CHUNKS):
-                        done = (BLOCKS - 1) * P
-                        nc.scalar.copy(out=zt_sb[c][:, :, 0 : done // PACK], in_=zt[c][:, 0:done].rearrange("v (p t) -> v t p", t=PACK))
-                if b == BLOCKS - 1:
-                    if a == 0:
-                        out_bank = psum.tile([P, V], F32, name="out_bank", tag="outb")
-                    done = (BLOCKS - 1) * P
-                    last = e == V
-                    for c in range(a // P, e // P):
-                        rest = nc.vector.tensor_copy if last else nc.scalar.copy
-                        rest(out=zt_sb[c][:, :, done // PACK : P], in_=zt[c][:, done:H].rearrange("v (p t) -> v t p", t=PACK))
-                        turn_back(c, back_tags[c], (nc.vector.tensor_copy, nc.scalar.copy) if last else (nc.scalar.copy,))
-                    for q0, q1 in QUANT[(a, e)]:
-                        finish(q0, q1, nc.vector.tensor_copy if last else nc.scalar.copy)
-                    nc.sync.dma_start(out=out[:, a:e], in_=out_sb[:, a:e])
+        for d in range(D):
+            gather(BLOCKS - 1, 0, SPLIT, d)
+        for c in range(SPLIT // P):
+            round_sums(nc.scalar.copy, c, done, H)
+            turn_back(c, back_tags[c], (nc.scalar.copy,))
+        for d in range(D):
+            gather(BLOCKS - 1, SPLIT, V, d)
+        for a, e in FIRST_QUANTS:
+            finish(a, e, nc.scalar.copy)
+        nc.sync.dma_start(out=out[:, 0:SPLIT], in_=out_sb[:, 0:SPLIT])
+        for c in range(SPLIT // P, CHUNKS):
+            round_sums(nc.vector.tensor_copy, c, done, H)
+            turn_back(c, back_tags[c], (nc.vector.tensor_copy, nc.scalar.copy))
+        finish(SPLIT, V, nc.vector.tensor_copy)
+        nc.sync.dma_start(out=out[:, SPLIT:V], in_=out_sb[:, SPLIT:V])

from contextlib import ExitStack

import concourse.mybir as mybir
from concourse.masks import make_identity

K, T, D, V, H, N = 2048, 1024, 6, 512, 512, 128
FLOPS = 2 * K * H * T + 2 * H * N * V
BYTES = 4 * (K * T + K * H + H * N + D * V + N * V) + 2 * D * 128 * (V // 16)

F32 = mybir.dt.float32
BF16 = mybir.dt.bfloat16
U32 = mybir.dt.uint32
U16 = mybir.dt.uint16
U8 = mybir.dt.uint8
FP8X4 = mybir.dt.float8_e4m3fn_x4
MULT = mybir.AluOpType.mult
GELU = mybir.ActivationFunctionType.Gelu_apprx_tanh

P = 128
PACK = 4
KP = P * PACK
PASSES = K // KP
BLOCKS = H // P
CHUNKS = V // P

LAST_PIECES = ((0, 512), (512, 768), (768, 896), (896, 1024))
BANK_COLS = LAST_PIECES
QUANTIZE_AFTER = {(0, 1): ((1, 0, 2),), (0, 2): ((1, 2, 2),), (1, 0): ((2, 0, 2),), (1, 2): ((2, 2, 2),)}
MULTIPLY_AFTER = {(0, 1): ((0, 2),), (0, 2): ((2, 2),), (1, 0): ((0, 2),), (1, 2): ((2, 2),), (2, 0): ((0, 4),)}
SPLIT = 384
FIRST_QUANTS = ((0, 256), (256, 384))


def tile_picked_gcn_mlp_gelu_sub_l_kernel(tc, xT, w1, w2, gate, pos1, pos2, pos3, pos4, pos5, pos6, out):
    nc = tc.nc
    lists = (pos1, pos2, pos3, pos4, pos5, pos6)

    def interleave(copy, dst, raw):
        copy(
            out=dst.rearrange("p (c i) j -> p c j i", i=4),
            in_=raw.rearrange("p j (c i) -> p c j i", i=4),
        )

    def quantize(codes, scales, bf):
        nc.vector.quantize_mx(out=codes.bitcast(FP8X4), scales=scales, in_=bf)

    with ExitStack() as ctx:
        keep = ctx.enter_context(tc.tile_pool(name="keep", bufs=1))
        stage = ctx.enter_context(tc.tile_pool(name="stage", bufs=3))
        gpool = ctx.enter_context(tc.tile_pool(name="gpool", bufs=8))
        psum = ctx.enter_context(tc.psum_pool(name="psum", bufs=1))

        offsets = [keep.tile([P, V // 16], U16, name=f"offsets{d}") for d in range(D)]
        ident = keep.tile([P, P], F32, name="ident")
        ident_bf = keep.tile([P, P], BF16, name="ident_bf")
        warm = keep.tile([P, 1], F32, name="warm")
        warm_out = keep.tile([P, 1], F32, name="warm_out")
        gate_rows = keep.tile([P, V], F32, name="gate_rows")
        gate_cols = keep.tile([P, CHUNKS, D], F32, name="gate_cols")
        gates = [keep.tile([P, V], F32, name=f"gate{d}") for d in range(D)]

        x_raw = [keep.tile([P, PACK, T], F32, name=f"x_raw{c}") for c in range(PASSES)]
        x_codes = [keep.tile([P, T], U32, name=f"x_codes{c}", align_bytes=64) for c in range(PASSES)]
        x_scales = [keep.tile([P, T], U8, name=f"x_scales{c}", align_bytes=64) for c in range(PASSES)]

        groups = ((0, 128), (128, 128), (256, 256))
        w1_raw = [[keep.tile([P, PACK, w], F32, name=f"w1_raw{g}_{c}") for c in range(PASSES)] for g, (a, w) in enumerate(groups)]
        w1_bf = [keep.tile([P, PASSES, w, PACK], BF16, name=f"w1_bf{g}", align_bytes=64) for g, (a, w) in enumerate(groups)]
        w1_codes = [keep.tile([P, PASSES, w], U32, name=f"w1_codes{g}", align_bytes=64) for g, (a, w) in enumerate(groups)]
        w1_scales = [keep.tile([P, PASSES, w], U8, name=f"w1_scales{g}", align_bytes=64) for g, (a, w) in enumerate(groups)]
        w2_raw = keep.tile([P, PACK, N], F32, name="w2_raw")
        w2_bf = keep.tile([P, N, PACK], BF16, name="w2_bf", align_bytes=64)
        w2_codes = keep.tile([P, N], U32, name="w2_codes", align_bytes=64)
        w2_scales = keep.tile([P, N], U8, name="w2_scales", align_bytes=64)
        zt_sb = [keep.tile([P, PACK, P], BF16, name=f"zt_sb{c}") for c in range(CHUNKS)]
        z_bf = keep.tile([P, V, PACK], BF16, name="z_bf", align_bytes=64)
        z_codes = keep.tile([P, V], U32, name="z_codes", align_bytes=64)
        z_scales = keep.tile([P, V], U8, name="z_scales", align_bytes=64)
        out_sb = keep.tile([P, V], F32, name="out_sb")

        def load_w1(g, c):
            a, w = groups[g]
            nc.sync.dma_start(out=w1_raw[g][c][:], in_=w1[c * KP : (c + 1) * KP, a : a + w].rearrange("(p j) i -> p j i", j=PACK))

        def load_x(c, a, b):
            nc.sync.dma_start(out=x_raw[c][:, :, a:b], in_=xT[c * KP : (c + 1) * KP, a:b].rearrange("(p j) t -> p j t", j=PACK))

        def load_list(d):
            nc.sync.dma_start(offsets[d][:], lists[d])

        nc.vector.memset(gate_rows[:], 0.0)
        nc.gpsimd.memset(warm[:], 0.0)
        nc.scalar.activation(out=warm_out[:], in_=warm[:], func=GELU)
        make_identity(nc, ident[:])
        nc.gpsimd.tensor_copy(out=ident_bf[:], in_=ident[:])

        for c in range(PASSES):
            load_w1(0, c)
        nc.sync.dma_start(out=gate_rows[0:4, :], in_=gate[0:4, 0, :])
        nc.sync.dma_start(out=gate_rows[4:6, :], in_=gate[4:6, 0, :])
        load_x(0, 0, T)
        load_x(1, 0, T)
        load_list(0)
        load_x(2, 0, T)
        for a, b in LAST_PIECES:
            load_x(3, a, b)
        load_w1(1, 0)
        load_w1(1, 1)
        load_list(1)
        load_w1(1, 2)
        load_list(2)
        load_w1(1, 3)
        for d in range(3, D):
            load_list(d)
        for c in range(PASSES):
            load_w1(2, c)
        nc.sync.dma_start(out=w2_raw[:], in_=w2.rearrange("(p j) m -> p j m", j=PACK))

        turned = psum.tile([P, CHUNKS, P], F32, name="turned", tag="zt0")
        for c in range(CHUNKS):
            nc.tensor.transpose(out=turned[:, c, :], in_=gate_rows[:, c * P : (c + 1) * P], identity=ident[:])
        nc.vector.tensor_copy(out=gate_cols[:], in_=turned[:, :, 0:D])
        for d in range(D):
            spread = psum.tile([P, CHUNKS, P], F32, name=f"spread{d}", tag=f"zt{(d + 1) % 4}")
            for c in range(CHUNKS):
                nc.tensor.transpose(out=spread[:, c, :], in_=gate_cols[:, c, d : d + 1].to_broadcast([P, P]), identity=ident[:])
            nc.scalar.copy(out=gates[d][:], in_=spread[:].rearrange("p c v -> p (c v)"))

        def quantize_w1(g, c0, n):
            cs = slice(c0, c0 + n)
            quantize(
                w1_codes[g][:, cs].rearrange("p c i -> p (c i)"),
                w1_scales[g][:, cs].rearrange("p c i -> p (c i)"),
                w1_bf[g][:, cs].rearrange("p c i j -> p (c i j)"),
            )

        def cast_w1(g):
            for c in range(PASSES):
                interleave(nc.scalar.copy, w1_bf[g][:, c], w1_raw[g][c][:])

        cast_w1(0)
        quantize_w1(0, 0, 2)
        quantize_w1(0, 2, 2)

        banks0 = [psum.tile([P, 512], F32, name=f"h0_{i}", tag=t) for i, t in enumerate(("hA", "hB", "back", "outb"))]

        def product(bank, width, g, off, c, a):
            nc.tensor.matmul_mx(
                out=bank[:, 0:width],
                lhsT=w1_codes[g][:, c, off : off + P].bitcast(FP8X4),
                lhsT_scale=w1_scales[g][:, c, off : off + P],
                rhs=x_codes[c][:, a : a + width].bitcast(FP8X4),
                rhs_scale=x_scales[c][:, a : a + width],
                start=(c == 0),
                stop=(c == PASSES - 1),
            )

        for c in range(PASSES):
            x_bf = stage.tile([P, T, PACK], BF16, name=f"x_bf{c}", tag="x_bf", align_bytes=64)
            flat = x_bf[:].rearrange("p t j -> p (t j)")
            if c < PASSES - 1:
                casts = ((nc.vector.tensor_copy, 0, 256), (nc.vector.tensor_copy, 256, 512), (nc.scalar.copy, 768, 1024), (nc.vector.tensor_copy, 512, 768))
                if c == 0:
                    casts = ((nc.vector.tensor_copy, 0, 256), (nc.scalar.copy, 256, 512), (nc.vector.tensor_copy, 512, 768), (nc.scalar.copy, 768, 1024))
                for copy, a, b in casts:
                    interleave(copy, x_bf[:, a:b, :], x_raw[c][:, :, a:b])
                for a, b in ((0, 512), (512, 1024)):
                    quantize(x_codes[c][:, a:b], x_scales[c][:, a:b], flat[:, PACK * a : PACK * b])
            else:
                for a, b in LAST_PIECES:
                    m = b if b - a == P else a + (b - a) * 5 // 8
                    interleave(nc.vector.tensor_copy, x_bf[:, a:m, :], x_raw[c][:, :, a:m])
                    if m < b:
                        interleave(nc.scalar.copy, x_bf[:, m:b, :], x_raw[c][:, :, m:b])
                    quantize(x_codes[c][:, a:b], x_scales[c][:, a:b], flat[:, PACK * a : PACK * b])
            for bank, (a, b) in zip(banks0, BANK_COLS):
                product(bank, b - a, 0, 0, c, a)

        h = [keep.tile([P, T], F32, name=f"h{b}") for b in range(BLOCKS)]
        for bank, (a, b) in zip(banks0, BANK_COLS):
            nc.scalar.activation(out=h[0][:, a:b], in_=bank[:, 0 : b - a], func=GELU)

        cast_w1(1)
        cast_w1(2)
        interleave(nc.scalar.copy, w2_bf[:], w2_raw[:])

        def start_block(b):
            return [psum.tile([P, 512], F32, name=f"h{b}_{i}", tag=t) for i, t in enumerate(("hA", "hB"))]

        def multiply_block(b, banks, c0, n):
            g, off = ((0, 0), (1, 0), (2, 0), (2, P))[b]
            for c in range(c0, c0 + n):
                for i, bank in enumerate(banks):
                    product(bank, 512, g, off, c, 512 * i)
                    if c == PASSES - 1:
                        nc.scalar.activation(out=h[b][:, 512 * i : 512 * (i + 1)], in_=bank[:], func=GELU)

        zt = [psum.tile([P, H], F32, name=f"zt_{c}", tag=f"zt{c}") for c in range(CHUNKS)]

        def turn_back(c, tag, copies):
            back = psum.tile([P, PACK, P], BF16, name=f"back{c}", tag=tag)
            for t in range(PACK):
                nc.tensor.transpose(out=back[:, t, :], in_=zt_sb[c][:, t, :], identity=ident_bf[:])
            step = P // len(copies)
            for i, copy in enumerate(copies):
                interleave(copy, z_bf[:, c * P + i * step : c * P + (i + 1) * step, :], back[:, :, i * step : (i + 1) * step])

        def finish(a, e, copy):
            quantize(z_codes[:, a:e], z_scales[:, a:e], z_bf[:, a:e, :].rearrange("p v j -> p (v j)"))
            nc.tensor.matmul_mx(
                out=out_bank[:, a:e],
                lhsT=w2_codes[:].bitcast(FP8X4),
                lhsT_scale=w2_scales[:],
                rhs=z_codes[:, a:e].bitcast(FP8X4),
                rhs_scale=z_scales[:, a:e],
                start=True,
                stop=True,
            )
            copy(out=out_sb[:, a:e], in_=out_bank[:, a:e])

        def gather(b, a, e, d):
            picked = gpool.tile([P, e - a], F32, name=f"picked{b}_{a}_{d}", tag="picked")
            offs = offsets[d][:] if e - a == V else offsets[d][:, a // 16 : e // 16]
            nc.vector.tensor_tensor(picked[:], h[b][:].indirect(offs), gates[d][:, a:e], MULT)
            for c in range(a // P, e // P):
                nc.tensor.matmul(
                    zt[c][:, b * P : (b + 1) * P],
                    picked[:, c * P - a : (c + 1) * P - a],
                    ident[:],
                    start=(d == 0),
                    stop=(d == D - 1),
                    is_transpose=True,
                )

        def round_sums(copy, c, a, e):
            copy(out=zt_sb[c][:, :, a // PACK : e // PACK], in_=zt[c][:, a:e].rearrange("v (p t) -> v t p", t=PACK))

        for b in range(BLOCKS - 1):
            nb = start_block(b + 1)
            for d in range(D):
                gather(b, 0, V, d)
                for g, c0, n in QUANTIZE_AFTER.get((b, d), ()):
                    quantize_w1(g, c0, n)
                for c0, n in MULTIPLY_AFTER.get((b, d), ()):
                    multiply_block(b + 1, nb, c0, n)
        quantize(w2_codes[:], w2_scales[:], w2_bf[:].rearrange("p m j -> p (m j)"))

        done = (BLOCKS - 1) * P
        for c in range(CHUNKS):
            round_sums(nc.scalar.copy, c, 0, done)
        out_bank = psum.tile([P, V], F32, name="out_bank", tag="outb")
        back_tags = ("back", "hA", "hB", "back")
        for d in range(D):
            gather(BLOCKS - 1, 0, SPLIT, d)
        for c in range(SPLIT // P):
            round_sums(nc.scalar.copy, c, done, H)
            turn_back(c, back_tags[c], (nc.scalar.copy,))
        for d in range(D):
            gather(BLOCKS - 1, SPLIT, V, d)
        for a, e in FIRST_QUANTS:
            finish(a, e, nc.scalar.copy)
        nc.sync.dma_start(out=out[:, 0:SPLIT], in_=out_sb[:, 0:SPLIT])
        for c in range(SPLIT // P, CHUNKS):
            round_sums(nc.vector.tensor_copy, c, done, H)
            turn_back(c, back_tags[c], (nc.vector.tensor_copy, nc.scalar.copy))
        finish(SPLIT, V, nc.vector.tensor_copy)
        nc.sync.dma_start(out=out[:, SPLIT:V], in_=out_sb[:, SPLIT:V])
